import numpy as np
import ml_dtypes


def mxq(x, axis, fmt="e4m3"):
    dtype, down = {"e4m3": (ml_dtypes.float8_e4m3fn, 7), "e5m2": (ml_dtypes.float8_e5m2, 14)}[fmt]
    v = np.moveaxis(np.asarray(x, np.float32).astype(ml_dtypes.bfloat16).astype(np.float64), axis, -1)
    blocks = v.reshape(v.shape[:-1] + (-1, 32))
    amax = np.abs(blocks).max(-1, keepdims=True)
    byte = np.maximum(np.where(amax > 0, np.frexp(amax)[1] - 1 + 127, 0) - down, 1)
    scale = np.exp2(byte - 127.0)
    codes = (blocks / scale).astype(np.float32).astype(dtype).astype(np.float64)
    return np.moveaxis((codes * scale).reshape(v.shape), -1, axis)


WIDE = False


def mx_kscale(k):
    if not WIDE:
        return np.ones(k)
    levels = np.array([10, -10, 5, -5, 0])
    if k % 512:
        return np.exp2(np.random.permutation(np.resize(levels, k // 32))).repeat(32)
    a = np.empty((k // 512, 16))
    for p in range(k // 512):
        a[p, :8] = np.random.permutation(np.resize(levels, 8))
        for g in range(8):
            far = levels[np.abs(levels - a[p, g]) >= 10]
            a[p, g + 8] = far[np.random.randint(len(far))]
    return np.exp2(a.ravel()).repeat(32)


def f64(x):
    return np.asarray(x).astype(np.float64)


def striped(idx):
    return np.tile(idx.reshape(-1, 16).T, (8, 1)).astype(np.uint16)


def unstriped(offs):
    return offs[:16].T.reshape(-1).astype(np.int64)


def pack_weight(w):
    k, n = w.shape
    w = f64(np.asarray(w, np.float32).astype(ml_dtypes.bfloat16)).reshape(k // 32, 32, n)
    amax = np.abs(w).max(1)
    byte = np.clip(np.where(amax > 0, np.frexp(amax)[1] - 1 + 127 - 7, 1), 1, 254)
    scaled = (w * np.exp2(127.0 - byte)[:, None, :]).reshape(k, n).astype(np.float32)
    words = np.ascontiguousarray(scaled.reshape(k // 512, 128, 4, n).transpose(0, 1, 3, 2)).astype(ml_dtypes.float8_e4m3fn).view(np.uint8)
    return words, np.ascontiguousarray(byte.astype(np.uint8).reshape(k // 512, 16, n))


def unpack_weight(words, scales):
    g, p, n, _ = words.shape
    vals = np.ascontiguousarray(words).view(ml_dtypes.float8_e4m3fn).astype(np.float64) * np.repeat(np.exp2(scales.astype(np.float64) - 127.0), 8, axis=1)[..., None]
    return vals.transpose(0, 1, 3, 2).reshape(g * 512, n)


def sigmoid(v):
    return 1.0 / (1.0 + np.exp(-np.maximum(v, -700.0)))


K, T, S, N, H = 512, 2048, 512, 256, 512


def setup_inputs():
    n = np.random.standard_normal
    s = mx_kscale(K)[:, None]
    u = mx_kscale(H)
    packed_xT = pack_weight(n((K, T)) * s)
    return {
        "x_words": packed_xT[0],
        "x_scales": packed_xT[1],
        "w1": (n((K, H)) / np.sqrt(K) / s).astype(np.float32),
        "w2": (n((K, H)) / np.sqrt(K) / s).astype(np.float32),
        "unit": (np.random.uniform(0.6, 1.4, (H, 1)) * u[:, None]).astype(np.float32),
        "w3": (n((H, N)) / np.sqrt(H) / u[:, None]).astype(np.float32),
        "offs": striped(np.random.permutation(T)[:S]),
        "s1": striped(np.random.permutation(S)),
        "s2": striped(np.random.permutation(S)),
    }


def reference(x_words, x_scales, w1, w2, unit, w3, offs, s1, s2):
    xq = unpack_weight(x_words, x_scales)[:, unstriped(offs)]
    yg = mxq(f64(w2), 0, "e4m3").T @ xq
    set1 = sigmoid(1.5 * yg)
    set2 = set1[:, unstriped(s2)]
    y = mxq(f64(w1), 0, "e4m3").T @ xq
    y1 = y[:, unstriped(s1)]
    lay1 = set1 * y + (-1.0 * set1 + 1.0) * y1
    x12 = lay1[:, unstriped(s2)]
    lay2 = set2 * lay1 + (-1.0 * set2 + 1.0) * x12
    hid = f64(unit) * lay2
    return mxq(f64(w3), 0, "e4m3").T @ mxq(hid, 0, "e4m3")

@@ -1,0 +1,154 @@
+from contextlib import ExitStack
+
+import concourse.mybir as mybir
+
+K, T, S, N, H = 512, 2048, 512, 256, 512
+FLOPS = 2 * K * H * S * 2 + 2 * H * N * S
+
+F32 = mybir.dt.float32
+BF16 = mybir.dt.bfloat16
+I32 = mybir.dt.int32
+U32 = mybir.dt.uint32
+U16 = mybir.dt.uint16
+U8 = mybir.dt.uint8
+FP8X4 = mybir.dt.float8_e4m3fn_x4
+ACT = mybir.ActivationFunctionType
+ALU = mybir.AluOpType
+
+P = 128
+PACK = 4
+HALF = S // 2
+LIST_HALF = HALF // 16
+
+
+def tile_picked_ybenesn_route_p_kernel(tc, x_words, x_scales, w1, w2, unit, w3, offs, s1, s2, out):
+    nc = tc.nc
+    with ExitStack() as ctx:
+        keep = ctx.enter_context(tc.tile_pool(name="keep", bufs=1))
+        psum = ctx.enter_context(tc.psum_pool(name="psum", bufs=1))
+
+        offs_t = keep.tile([P, S // 16], U16, name="offs_t")
+        s1_t = keep.tile([P, S // 16], U16, name="s1_t")
+        s2_t = keep.tile([P, S // 16], U16, name="s2_t")
+        unit_t = keep.tile([P, PACK], F32, name="unit_t")
+        table_words = keep.tile([P, T], U32, name="table_words", align_bytes=64)
+        table_scales = keep.tile([P, T], U8, name="table_scales", align_bytes=64)
+        x_codes = keep.tile([P, S], U32, name="x_codes", align_bytes=64)
+        x_plane = keep.tile([P, S], U8, name="x_plane", align_bytes=64)
+
+        def load_half(w, name, h):
+            raw = keep.tile([P, PACK, H // 2], F32, name=name + "_raw%d" % h)
+            nc.sync.dma_start(raw[:], w.rearrange("(p j) c -> p j c", j=PACK)[:, :, h * (H // 2) : (h + 1) * (H // 2)])
+            return raw
+
+        nc.vector.memset(table_scales[:].bitcast(I32), 0)
+        for q in range(4):
+            nc.scalar.dma_start(table_scales[32 * q : 32 * q + 4, :].bitcast(I32), x_scales[0, 4 * q : 4 * q + 4, :].bitcast(I32))
+        nc.sync.dma_start(offs_t[:], offs)
+        nc.sync.dma_start(s1_t[:], s1)
+        nc.sync.dma_start(s2_t[:], s2)
+        nc.sync.dma_start(unit_t[:], unit.rearrange("(p t) o -> p (t o)", t=PACK))
+        w2_raw = [load_half(w2, "w2", h) for h in range(2)]
+        nc.sync.dma_start(table_words[:].bitcast(I32), x_words[0].rearrange("p n t -> p (n t)").bitcast(I32))
+        w1_raw = [load_half(w1, "w1", h) for h in range(2)]
+
+        def deal(raw, name, copies):
+            dealt = keep.tile([P, PACK * H], BF16, name=name + "_dealt", align_bytes=64)
+            dealt_view = dealt[:].rearrange("p (t m j) -> p m j t", t=PACK, j=PACK)
+            for h in range(2):
+                copies[h](dealt_view[:, h * 64 : (h + 1) * 64], raw[h][:].rearrange("p j (m t) -> p m j t", t=PACK))
+            return dealt
+
+        def quantise(dealt, name, pieces):
+            codes = keep.tile([P, H], U32, name=name + "_codes", align_bytes=64)
+            plane = keep.tile([P, H], U8, name=name + "_plane", align_bytes=64)
+            width = H // pieces
+            for i in range(pieces):
+                cols = slice(i * width, (i + 1) * width)
+                nc.vector.quantize_mx(out=codes[:, cols].bitcast(FP8X4), scales=plane[:, cols], in_=dealt[:, i * PACK * width : (i + 1) * PACK * width])
+            return codes, plane
+
+        def product(codes, plane, name):
+            banks = []
+            for t in range(PACK):
+                cols = slice(t * P, (t + 1) * P)
+                bank = psum.tile([P, S], F32, name=name + "_bank", tag=name + "_bank%d" % t)
+                nc.tensor.matmul_mx(out=bank[:], lhsT=codes[:, cols].bitcast(FP8X4), lhsT_scale=plane[:, cols],
+                                    rhs=x_codes[:].bitcast(FP8X4), rhs_scale=x_plane[:], start=True, stop=True)
+                banks.append(bank)
+            return banks
+
+        halves = [(slice(h * HALF, (h + 1) * HALF), slice(h * LIST_HALF, (h + 1) * LIST_HALF)) for h in range(2)]
+
+        w2_q = quantise(deal(w2_raw, "w2", [nc.scalar.copy, nc.vector.tensor_copy]), "w2", 1)
+        w3_raw = keep.tile([P, PACK, N], F32, name="w3_raw", tag="w2_raw0")
+        nc.sync.dma_start(w3_raw[:], w3.rearrange("(p j) n -> p j n", j=PACK))
+        nc.vector.tensor_copy(x_plane[:], table_scales[:].indirect(offs_t[:]))
+        nc.vector.tensor_copy(x_codes[:], table_words[:].indirect(offs_t[:]))
+        g_banks = product(w2_q[0], w2_q[1], "w2")
+        set1 = []
+        for t in range(PACK):
+            set1.append(keep.tile([P, S], F32, name="set1_%d" % t))
+            nc.scalar.activation(set1[t][:], g_banks[t][:], ACT.Sigmoid, scale=1.5)
+
+        w1_q = quantise(deal(w1_raw, "w1", [nc.vector.tensor_copy, nc.vector.tensor_copy]), "w1", 4)
+        y_banks = product(w1_q[0], w1_q[1], "w1")
+
+        lay1 = []
+        for t in range(PACK):
+            y = keep.tile([P, S], F32, name="y%d" % t)
+            y1 = keep.tile([P, S], F32, name="y1_%d" % t)
+            d = keep.tile([P, S], F32, name="d%d" % t)
+            m = keep.tile([P, S], F32, name="m%d" % t)
+            lay1.append(keep.tile([P, S], F32, name="lay1_%d" % t))
+            if t == 0:
+                nc.vector.tensor_scalar(y[:], y_banks[t][:], unit_t[:, t : t + 1], None, ALU.mult)
+                for cols, entries in halves:
+                    nc.vector.tensor_copy(y1[:, cols], y[:].indirect(s1_t[:, entries]))
+            else:
+                nc.scalar.activation(y[:], y_banks[t][:], ACT.Copy, scale=unit_t[:, t : t + 1])
+                for cols, entries in halves:
+                    nc.scalar.activation(y1[:, cols], y[:].indirect(s1_t[:, entries]), ACT.Copy)
+            nc.vector.tensor_tensor(d[:], y[:], y1[:], ALU.subtract)
+            nc.vector.tensor_tensor(m[:], d[:], set1[t][:], ALU.mult)
+            nc.vector.tensor_tensor(lay1[t][:], m[:], y1[:], ALU.add)
+
+        x12 = keep.tile([P, PACK, S], F32, name="x12")
+        f = keep.tile([P, PACK, S], F32, name="f")
+        for t in range(PACK):
+            e = keep.tile([P, S], F32, name="e%d" % t)
+            for cols, entries in halves:
+                nc.scalar.activation(x12[:, t, cols], lay1[t][:].indirect(s2_t[:, entries]), ACT.Copy)
+            nc.vector.tensor_tensor(e[:], lay1[t][:], x12[:, t, :], ALU.subtract)
+            if t in (0,):
+                for cols, entries in halves:
+                    nc.vector.tensor_tensor(f[:, t, cols], set1[t][:].indirect(s2_t[:, entries]), e[:, cols], ALU.mult)
+            else:
+                set2 = keep.tile([P, S], F32, name="set2_%d" % t, tag="m%d" % t)
+                for cols, entries in halves:
+                    nc.scalar.activation(set2[:, cols], set1[t][:].indirect(s2_t[:, entries]), ACT.Copy)
+                nc.vector.tensor_tensor(f[:, t, :], e[:], set2[:], ALU.mult)
+
+        w3_grouped = keep.tile([P, PACK * N], BF16, name="w3_grouped", align_bytes=64)
+        w3_codes = keep.tile([P, N], U32, name="w3_codes", align_bytes=64)
+        w3_plane = keep.tile([P, N], U8, name="w3_plane", align_bytes=64)
+        nc.vector.tensor_copy(w3_grouped[:].rearrange("p (c i t) -> p c t i", i=4, t=PACK),
+                              w3_raw[:].rearrange("p t (c i) -> p c t i", i=4))
+        nc.vector.quantize_mx(out=w3_codes[:].bitcast(FP8X4), scales=w3_plane[:], in_=w3_grouped[:])
+
+        for h, (cols, entries) in enumerate(halves):
+            hid = keep.tile([P, PACK * HALF], BF16, name="hid%d" % h, align_bytes=64)
+            h_codes = keep.tile([P, HALF], U32, name="h_codes%d" % h, align_bytes=64)
+            h_plane = keep.tile([P, HALF], U8, name="h_plane%d" % h, align_bytes=64)
+            nc.vector.tensor_tensor(hid[:].rearrange("p (c i t) -> p c t i", i=4, t=PACK),
+                                    f[:, :, cols].rearrange("p t (c i) -> p c t i", i=4),
+                                    x12[:, :, cols].rearrange("p t (c i) -> p c t i", i=4), ALU.add)
+            nc.vector.quantize_mx(out=h_codes[:].bitcast(FP8X4), scales=h_plane[:], in_=hid[:])
+            bank = psum.tile([P, 2, HALF], F32, name="out_bank", tag="w2_bank%d" % h)
+            for a in range(2):
+                rows = slice(a * P, (a + 1) * P)
+                nc.tensor.matmul_mx(out=bank[:, a, :], lhsT=w3_codes[:, rows].bitcast(FP8X4), lhsT_scale=w3_plane[:, rows],
+                                    rhs=h_codes[:].bitcast(FP8X4), rhs_scale=h_plane[:], start=True, stop=True)
+            res = keep.tile([P, 2, HALF], F32, name="res%d" % h)
+            nc.scalar.copy(res[:], bank[:])
+            nc.sync.dma_start(out.rearrange("(a p) j -> p a j", p=P)[:, :, cols], res[:])

@@ -19,6 +19,7 @@ P = 128
 PACK = 4
 HALF = S // 2
 LIST_HALF = HALF // 16
+WIN = S + 16
 
 
 def tile_picked_ybenesn_route_p_kernel(tc, x_words, x_scales, w1, w2, unit, w3, offs, s1, s2, out):
@@ -54,9 +55,9 @@ def tile_picked_ybenesn_route_p_kernel(tc, x_words, x_scales, w1, w2, unit, w3, 
 
         def deal(raw, name, copies):
             dealt = keep.tile([P, PACK * H], BF16, name=name + "_dealt", align_bytes=64)
-            dealt_view = dealt[:].rearrange("p (t m j) -> p m j t", t=PACK, j=PACK)
+            dealt_view = dealt[:].rearrange("p (t m j) -> p m t j", t=PACK, j=PACK)
             for h in range(2):
-                copies[h](dealt_view[:, h * 64 : (h + 1) * 64], raw[h][:].rearrange("p j (m t) -> p m j t", t=PACK))
+                copies[h](dealt_view[:, h * 64 : (h + 1) * 64], raw[h][:].rearrange("p j (m t) -> p m t j", t=PACK))
             return dealt
 
         def quantise(dealt, name, pieces):
@@ -80,53 +81,49 @@ def tile_picked_ybenesn_route_p_kernel(tc, x_words, x_scales, w1, w2, unit, w3, 
 
         halves = [(slice(h * HALF, (h + 1) * HALF), slice(h * LIST_HALF, (h + 1) * LIST_HALF)) for h in range(2)]
 
+        nc.vector.tensor_copy(x_plane[:], table_scales[:].indirect(offs_t[:]))
         w2_q = quantise(deal(w2_raw, "w2", [nc.scalar.copy, nc.vector.tensor_copy]), "w2", 1)
         w3_raw = keep.tile([P, PACK, N], F32, name="w3_raw", tag="w2_raw0")
         nc.sync.dma_start(w3_raw[:], w3.rearrange("(p j) n -> p j n", j=PACK))
-        nc.vector.tensor_copy(x_plane[:], table_scales[:].indirect(offs_t[:]))
         nc.vector.tensor_copy(x_codes[:], table_words[:].indirect(offs_t[:]))
         g_banks = product(w2_q[0], w2_q[1], "w2")
         set1 = []
         for t in range(PACK):
-            set1.append(keep.tile([P, S], F32, name="set1_%d" % t))
-            nc.scalar.activation(set1[t][:], g_banks[t][:], ACT.Sigmoid, scale=1.5)
+            set1.append(keep.tile([P, WIN], F32, name="set1_%d" % t))
+            nc.scalar.activation(set1[t][:, :S], g_banks[t][:], ACT.Sigmoid, scale=1.5)
 
-        w1_q = quantise(deal(w1_raw, "w1", [nc.vector.tensor_copy, nc.vector.tensor_copy]), "w1", 4)
+        w1_q = quantise(deal(w1_raw, "w1", [nc.vector.tensor_copy, nc.vector.tensor_copy]), "w1", 2)
         y_banks = product(w1_q[0], w1_q[1], "w1")
 
         lay1 = []
         for t in range(PACK):
-            y = keep.tile([P, S], F32, name="y%d" % t)
+            y = keep.tile([P, WIN], F32, name="y%d" % t)
             y1 = keep.tile([P, S], F32, name="y1_%d" % t)
             d = keep.tile([P, S], F32, name="d%d" % t)
             m = keep.tile([P, S], F32, name="m%d" % t)
-            lay1.append(keep.tile([P, S], F32, name="lay1_%d" % t))
+            lay1.append(keep.tile([P, WIN], F32, name="lay1_%d" % t))
             if t == 0:
-                nc.vector.tensor_scalar(y[:], y_banks[t][:], unit_t[:, t : t + 1], None, ALU.mult)
+                nc.vector.tensor_scalar(y[:, :S], y_banks[t][:], unit_t[:, t : t + 1], None, ALU.mult)
                 for cols, entries in halves:
                     nc.vector.tensor_copy(y1[:, cols], y[:].indirect(s1_t[:, entries]))
             else:
-                nc.scalar.activation(y[:], y_banks[t][:], ACT.Copy, scale=unit_t[:, t : t + 1])
-                for cols, entries in halves:
-                    nc.scalar.activation(y1[:, cols], y[:].indirect(s1_t[:, entries]), ACT.Copy)
-            nc.vector.tensor_tensor(d[:], y[:], y1[:], ALU.subtract)
-            nc.vector.tensor_tensor(m[:], d[:], set1[t][:], ALU.mult)
-            nc.vector.tensor_tensor(lay1[t][:], m[:], y1[:], ALU.add)
+                nc.scalar.activation(y[:, :S], y_banks[t][:], ACT.Copy, scale=unit_t[:, t : t + 1])
+                nc.scalar.activation(y1[:], y[:].indirect(s1_t[:]), ACT.Copy)
+            nc.vector.tensor_tensor(d[:], y[:, :S], y1[:], ALU.subtract)
+            nc.vector.tensor_tensor(m[:], d[:], set1[t][:, :S], ALU.mult)
+            nc.vector.tensor_tensor(lay1[t][:, :S], m[:], y1[:], ALU.add)
 
         x12 = keep.tile([P, PACK, S], F32, name="x12")
         f = keep.tile([P, PACK, S], F32, name="f")
         for t in range(PACK):
             e = keep.tile([P, S], F32, name="e%d" % t)
-            for cols, entries in halves:
-                nc.scalar.activation(x12[:, t, cols], lay1[t][:].indirect(s2_t[:, entries]), ACT.Copy)
-            nc.vector.tensor_tensor(e[:], lay1[t][:], x12[:, t, :], ALU.subtract)
-            if t in (0,):
-                for cols, entries in halves:
-                    nc.vector.tensor_tensor(f[:, t, cols], set1[t][:].indirect(s2_t[:, entries]), e[:, cols], ALU.mult)
+            nc.scalar.activation(x12[:, t, :], lay1[t][:].indirect(s2_t[:]), ACT.Copy)
+            nc.vector.tensor_tensor(e[:], lay1[t][:, :S], x12[:, t, :], ALU.subtract)
+            if t == 0:
+                nc.vector.tensor_tensor(f[:, t, :], set1[t][:].indirect(s2_t[:]), e[:], ALU.mult)
             else:
                 set2 = keep.tile([P, S], F32, name="set2_%d" % t, tag="m%d" % t)
-                for cols, entries in halves:
-                    nc.scalar.activation(set2[:, cols], set1[t][:].indirect(s2_t[:, entries]), ACT.Copy)
+                nc.scalar.activation(set2[:], set1[t][:].indirect(s2_t[:]), ACT.Copy)
                 nc.vector.tensor_tensor(f[:, t, :], e[:], set2[:], ALU.mult)
 
         w3_grouped = keep.tile([P, PACK * N], BF16, name="w3_grouped", align_bytes=64)
@@ -136,19 +133,20 @@ def tile_picked_ybenesn_route_p_kernel(tc, x_words, x_scales, w1, w2, unit, w3, 
                               w3_raw[:].rearrange("p t (c i) -> p c t i", i=4))
         nc.vector.quantize_mx(out=w3_codes[:].bitcast(FP8X4), scales=w3_plane[:], in_=w3_grouped[:])
 
-        for h, (cols, entries) in enumerate(halves):
-            hid = keep.tile([P, PACK * HALF], BF16, name="hid%d" % h, align_bytes=64)
-            h_codes = keep.tile([P, HALF], U32, name="h_codes%d" % h, align_bytes=64)
-            h_plane = keep.tile([P, HALF], U8, name="h_plane%d" % h, align_bytes=64)
+        for h, (start, width) in enumerate(((0, 256), (256, 128), (384, 128))):
+            cols = slice(start, start + width)
+            hid = keep.tile([P, PACK * width], BF16, name="hid%d" % h, align_bytes=64)
+            h_codes = keep.tile([P, width], U32, name="h_codes%d" % h, align_bytes=64)
+            h_plane = keep.tile([P, width], U8, name="h_plane%d" % h, align_bytes=64)
             nc.vector.tensor_tensor(hid[:].rearrange("p (c i t) -> p c t i", i=4, t=PACK),
                                     f[:, :, cols].rearrange("p t (c i) -> p c t i", i=4),
                                     x12[:, :, cols].rearrange("p t (c i) -> p c t i", i=4), ALU.add)
             nc.vector.quantize_mx(out=h_codes[:].bitcast(FP8X4), scales=h_plane[:], in_=hid[:])
-            bank = psum.tile([P, 2, HALF], F32, name="out_bank", tag="w2_bank%d" % h)
+            bank = psum.tile([P, 2, width], F32, name="out_bank", tag="w2_bank%d" % h)
             for a in range(2):
                 rows = slice(a * P, (a + 1) * P)
                 nc.tensor.matmul_mx(out=bank[:, a, :], lhsT=w3_codes[:, rows].bitcast(FP8X4), lhsT_scale=w3_plane[:, rows],
                                     rhs=h_codes[:].bitcast(FP8X4), rhs_scale=h_plane[:], start=True, stop=True)
-            res = keep.tile([P, 2, HALF], F32, name="res%d" % h)
+            res = keep.tile([P, 2, width], F32, name="res%d" % h)
             nc.scalar.copy(res[:], bank[:])
             nc.sync.dma_start(out.rearrange("(a p) j -> p a j", p=P)[:, :, cols], res[:])

@@ -44,14 +44,15 @@ def tile_picked_ybenesn_route_p_kernel(tc, x_words, x_scales, w1, w2, unit, w3, 
 
         nc.vector.memset(table_scales[:].bitcast(I32), 0)
         for q in range(4):
-            nc.scalar.dma_start(table_scales[32 * q : 32 * q + 4, :].bitcast(I32), x_scales[0, 4 * q : 4 * q + 4, :].bitcast(I32))
+            nc.sync.dma_start(table_scales[32 * q : 32 * q + 4, :].bitcast(I32), x_scales[0, 4 * q : 4 * q + 4, :].bitcast(I32))
+        w2_raw = [load_half(w2, "w2", 0)]
         nc.sync.dma_start(offs_t[:], offs)
-        nc.sync.dma_start(s1_t[:], s1)
-        nc.sync.dma_start(s2_t[:], s2)
-        nc.sync.dma_start(unit_t[:], unit.rearrange("(p t) o -> p (t o)", t=PACK))
-        w2_raw = [load_half(w2, "w2", h) for h in range(2)]
+        w2_raw.append(load_half(w2, "w2", 1))
         nc.sync.dma_start(table_words[:].bitcast(I32), x_words[0].rearrange("p n t -> p (n t)").bitcast(I32))
         w1_raw = [load_half(w1, "w1", h) for h in range(2)]
+        nc.sync.dma_start(unit_t[:], unit.rearrange("(p t) o -> p (t o)", t=PACK))
+        nc.sync.dma_start(s1_t[:], s1)
+        nc.sync.dma_start(s2_t[:], s2)
 
         def deal(raw, name, copies):
             dealt = keep.tile([P, PACK * H], BF16, name=name + "_dealt", align_bytes=64)
@@ -81,10 +82,10 @@ def tile_picked_ybenesn_route_p_kernel(tc, x_words, x_scales, w1, w2, unit, w3, 
 
         halves = [(slice(h * HALF, (h + 1) * HALF), slice(h * LIST_HALF, (h + 1) * LIST_HALF)) for h in range(2)]
 
-        nc.vector.tensor_copy(x_plane[:], table_scales[:].indirect(offs_t[:]))
         w2_q = quantise(deal(w2_raw, "w2", [nc.scalar.copy, nc.vector.tensor_copy]), "w2", 1)
         w3_raw = keep.tile([P, PACK, N], F32, name="w3_raw", tag="w2_raw0")
         nc.sync.dma_start(w3_raw[:], w3.rearrange("(p j) n -> p j n", j=PACK))
+        nc.vector.tensor_copy(x_plane[:], table_scales[:].indirect(offs_t[:]))
         nc.vector.tensor_copy(x_codes[:], table_words[:].indirect(offs_t[:]))
         g_banks = product(w2_q[0], w2_q[1], "w2")
         set1 = []

@@ -20,6 +20,7 @@ PACK = 4
 HALF = S // 2
 LIST_HALF = HALF // 16
 WIN = S + 16
+FUSED = 2
 
 
 def tile_picked_ybenesn_route_p_kernel(tc, x_words, x_scales, w1, w2, unit, w3, offs, s1, s2, out):
@@ -96,58 +97,109 @@ def tile_picked_ybenesn_route_p_kernel(tc, x_words, x_scales, w1, w2, unit, w3, 
         w1_q = quantise(deal(w1_raw, "w1", [nc.vector.tensor_copy, nc.vector.tensor_copy]), "w1", 2)
         y_banks = product(w1_q[0], w1_q[1], "w1")
 
-        lay1 = []
-        for t in range(PACK):
-            y = keep.tile([P, WIN], F32, name="y%d" % t)
-            y1 = keep.tile([P, S], F32, name="y1_%d" % t)
-            d = keep.tile([P, S], F32, name="d%d" % t)
-            m = keep.tile([P, S], F32, name="m%d" % t)
-            lay1.append(keep.tile([P, WIN], F32, name="lay1_%d" % t))
-            if t == 0:
-                nc.vector.tensor_scalar(y[:, :S], y_banks[t][:], unit_t[:, t : t + 1], None, ALU.mult)
-                for cols, entries in halves:
-                    nc.vector.tensor_copy(y1[:, cols], y[:].indirect(s1_t[:, entries]))
-            else:
-                nc.scalar.activation(y[:, :S], y_banks[t][:], ACT.Copy, scale=unit_t[:, t : t + 1])
-                nc.scalar.activation(y1[:], y[:].indirect(s1_t[:]), ACT.Copy)
-            nc.vector.tensor_tensor(d[:], y[:, :S], y1[:], ALU.subtract)
-            nc.vector.tensor_tensor(m[:], d[:], set1[t][:, :S], ALU.mult)
-            nc.vector.tensor_tensor(lay1[t][:, :S], m[:], y1[:], ALU.add)
-
-        x12 = keep.tile([P, PACK, S], F32, name="x12")
-        f = keep.tile([P, PACK, S], F32, name="f")
-        for t in range(PACK):
-            e = keep.tile([P, S], F32, name="e%d" % t)
-            nc.scalar.activation(x12[:, t, :], lay1[t][:].indirect(s2_t[:]), ACT.Copy)
-            nc.vector.tensor_tensor(e[:], lay1[t][:, :S], x12[:, t, :], ALU.subtract)
-            if t == 0:
-                nc.vector.tensor_tensor(f[:, t, :], set1[t][:].indirect(s2_t[:]), e[:], ALU.mult)
-            else:
-                set2 = keep.tile([P, S], F32, name="set2_%d" % t, tag="m%d" % t)
-                nc.scalar.activation(set2[:], set1[t][:].indirect(s2_t[:]), ACT.Copy)
-                nc.vector.tensor_tensor(f[:, t, :], e[:], set2[:], ALU.mult)
-
         w3_grouped = keep.tile([P, PACK * N], BF16, name="w3_grouped", align_bytes=64)
         w3_codes = keep.tile([P, N], U32, name="w3_codes", align_bytes=64)
         w3_plane = keep.tile([P, N], U8, name="w3_plane", align_bytes=64)
         nc.vector.tensor_copy(w3_grouped[:].rearrange("p (c i t) -> p c t i", i=4, t=PACK),
                               w3_raw[:].rearrange("p t (c i) -> p c t i", i=4))
+
+        y = [keep.tile([P, WIN], F32, name="y%d" % t) for t in range(PACK)]
+        y1 = [keep.tile([P, S], F32, name="y1_%d" % t) for t in range(PACK)]
+        own = [keep.tile([P, S], F32, name="own%d" % t) for t in range(PACK)]
+        taken = [keep.tile([P, S], F32, name="taken%d" % t) for t in range(PACK)]
+        lay1 = [keep.tile([P, S], F32, name="lay1_%d" % t) for t in range(PACK)]
+        offered = [keep.tile([P, S], F32, name="offered%d" % t) for t in range(PACK)]
+
+        def copy_y(t):
+            nc.scalar.activation(y[t][:, :S], y_banks[t][:], ACT.Copy, scale=unit_t[:, t : t + 1])
+
+        def fetch_y(t):
+            nc.scalar.activation(y1[t][:], y[t][:].indirect(s1_t[:]), ACT.Copy)
+
+        def make_own(t):
+            nc.vector.scalar_tensor_tensor(own[t][:], y_banks[t][:], unit_t[:, t : t + 1], set1[t][:, :S], ALU.mult, ALU.mult)
+
+        def make_taken(t):
+            nc.vector.scalar_tensor_tensor(taken[t][:], set1[t][:, :S], 1.0, y1[t][:], ALU.subtract, ALU.mult)
+
+        def make_lay1(t):
+            nc.vector.tensor_tensor(lay1[t][:], own[t][:], taken[t][:], ALU.subtract)
+
+        def make_offered(t):
+            nc.vector.scalar_tensor_tensor(offered[t][:], set1[t][:, :S], 1.0, lay1[t][:], ALU.subtract, ALU.mult)
+
+        make_own(2)
+        make_own(3)
+        copy_y(0)
+        copy_y(1)
+        make_own(0)
+        make_own(1)
+        for t in range(PACK):
+            fetch_y(t)
+            if t + 2 < PACK:
+                copy_y(t + 2)
+        make_taken(0)
         nc.vector.quantize_mx(out=w3_codes[:].bitcast(FP8X4), scales=w3_plane[:], in_=w3_grouped[:])
 
-        for h, (start, width) in enumerate(((0, 256), (256, 128), (384, 128))):
+        make_lay1(0)
+        for t in range(1, PACK):
+            make_taken(t)
+            make_offered(t - 1)
+            make_lay1(t)
+
+        kept = [keep.tile([P, PACK, HALF], F32, name="kept%d" % h) for h in range(2)]
+        fetched = [keep.tile([P, PACK, HALF], F32, name="fetched0"), keep.tile([P, PACK, HALF], F32, name="fetched1", tag="own3")]
+        set2 = {t: keep.tile([P, S], F32, name="set2_%d" % t, tag="taken%d" % (t - FUSED)) for t in range(FUSED, PACK)}
+
+        def make_kept(t, h):
+            cols, entries = halves[h]
+            if t < FUSED:
+                nc.vector.tensor_tensor(kept[h][:, t, :], set1[t][:].indirect(s2_t[:, entries]), lay1[t][:, cols], ALU.mult)
+            else:
+                nc.vector.tensor_tensor(kept[h][:, t, :], set2[t][:, cols], lay1[t][:, cols], ALU.mult)
+
+        def fetch_offered(t, h):
+            nc.scalar.activation(fetched[h][:, t, :], offered[t][:].indirect(s2_t[:, halves[h][1]]), ACT.Copy)
+
+        for t in range(FUSED, PACK):
+            nc.scalar.activation(set2[t][:], set1[t][:].indirect(s2_t[:]), ACT.Copy)
+        make_kept(0, 0)
+        make_offered(PACK - 1)
+        for h in range(2):
+            for t in range(PACK):
+                fetch_offered(t, h)
+        for h in range(2):
+            for t in range(PACK):
+                if (t, h) != (0, 0):
+                    make_kept(t, h)
+
+        chunks = ((0, 0, 256), (1, 0, 128), (1, 128, 128))
+        hid = [keep.tile([P, PACK * width], BF16, name="hid%d" % c, align_bytes=64) for c, (h, start, width) in enumerate(chunks)]
+
+        def make_hid(c):
+            h, start, width = chunks[c]
             cols = slice(start, start + width)
-            hid = keep.tile([P, PACK * width], BF16, name="hid%d" % h, align_bytes=64)
-            h_codes = keep.tile([P, width], U32, name="h_codes%d" % h, align_bytes=64)
-            h_plane = keep.tile([P, width], U8, name="h_plane%d" % h, align_bytes=64)
-            nc.vector.tensor_tensor(hid[:].rearrange("p (c i t) -> p c t i", i=4, t=PACK),
-                                    f[:, :, cols].rearrange("p t (c i) -> p c t i", i=4),
-                                    x12[:, :, cols].rearrange("p t (c i) -> p c t i", i=4), ALU.add)
-            nc.vector.quantize_mx(out=h_codes[:].bitcast(FP8X4), scales=h_plane[:], in_=hid[:])
-            bank = psum.tile([P, 2, width], F32, name="out_bank", tag="w2_bank%d" % h)
+            nc.vector.tensor_tensor(hid[c][:].rearrange("p (c i t) -> p c t i", i=4, t=PACK),
+                                    kept[h][:, :, cols].rearrange("p t (c i) -> p c t i", i=4),
+                                    fetched[h][:, :, cols].rearrange("p t (c i) -> p c t i", i=4), ALU.subtract)
+
+        def finish(c):
+            h, start, width = chunks[c]
+            cols = slice(h * HALF + start, h * HALF + start + width)
+            h_codes = keep.tile([P, width], U32, name="h_codes%d" % c, align_bytes=64)
+            h_plane = keep.tile([P, width], U8, name="h_plane%d" % c, align_bytes=64)
+            nc.vector.quantize_mx(out=h_codes[:].bitcast(FP8X4), scales=h_plane[:], in_=hid[c][:])
+            bank = psum.tile([P, 2, width], F32, name="out_bank", tag="w2_bank%d" % c)
             for a in range(2):
                 rows = slice(a * P, (a + 1) * P)
                 nc.tensor.matmul_mx(out=bank[:, a, :], lhsT=w3_codes[:, rows].bitcast(FP8X4), lhsT_scale=w3_plane[:, rows],
                                     rhs=h_codes[:].bitcast(FP8X4), rhs_scale=h_plane[:], start=True, stop=True)
-            res = keep.tile([P, 2, width], F32, name="res%d" % h)
+            res = keep.tile([P, 2, width], F32, name="res%d" % c)
             nc.scalar.copy(res[:], bank[:])
             nc.sync.dma_start(out.rearrange("(a p) j -> p a j", p=P)[:, :, cols], res[:])
+
+        make_hid(0)
+        for c in range(1, len(chunks)):
+            make_hid(c)
+            finish(c - 1)
+        finish(len(chunks) - 1)

@@ -17,10 +17,15 @@ ALU = mybir.AluOpType
 
 P = 128
 PACK = 4
+BLOCK = 32
+QUADRANT = 32
+PER_COLUMN = 16
+RUN = 4
 HALF = S // 2
-LIST_HALF = HALF // 16
-WIN = S + 16
+WINDOW = S + PER_COLUMN
 FUSED = 2
+LAST = 128
+CHUNKS = ((0, HALF), (HALF, HALF - LAST), (S - LAST, LAST))
 
 
 def tile_picked_ybenesn_route_p_kernel(tc, x_words, x_scales, w1, w2, unit, w3, offs, s1, s2, out):
@@ -29,81 +34,84 @@ def tile_picked_ybenesn_route_p_kernel(tc, x_words, x_scales, w1, w2, unit, w3, 
         keep = ctx.enter_context(tc.tile_pool(name="keep", bufs=1))
         psum = ctx.enter_context(tc.psum_pool(name="psum", bufs=1))
 
-        offs_t = keep.tile([P, S // 16], U16, name="offs_t")
-        s1_t = keep.tile([P, S // 16], U16, name="s1_t")
-        s2_t = keep.tile([P, S // 16], U16, name="s2_t")
+        offs_t = keep.tile([P, S // PER_COLUMN], U16, name="offs_t")
+        s1_t = keep.tile([P, S // PER_COLUMN], U16, name="s1_t")
+        s2_t = keep.tile([P, S // PER_COLUMN], U16, name="s2_t")
         unit_t = keep.tile([P, PACK], F32, name="unit_t")
         table_words = keep.tile([P, T], U32, name="table_words", align_bytes=64)
         table_scales = keep.tile([P, T], U8, name="table_scales", align_bytes=64)
         x_codes = keep.tile([P, S], U32, name="x_codes", align_bytes=64)
-        x_plane = keep.tile([P, S], U8, name="x_plane", align_bytes=64)
+        x_picked_scales = keep.tile([P, S], U8, name="x_picked_scales", align_bytes=64)
 
-        def load_half(w, name, h):
-            raw = keep.tile([P, PACK, H // 2], F32, name=name + "_raw%d" % h)
-            nc.sync.dma_start(raw[:], w.rearrange("(p j) c -> p j c", j=PACK)[:, :, h * (H // 2) : (h + 1) * (H // 2)])
+        def load_row_pair(w, name, h):
+            raw = keep.tile([P, 2, H], F32, name=name + "_raw%d" % h)
+            nc.sync.dma_start(raw[:], w.rearrange("(p j) c -> p j c", j=PACK)[:, 2 * h : 2 * h + 2, :])
             return raw
 
         nc.vector.memset(table_scales[:].bitcast(I32), 0)
-        for q in range(4):
-            nc.sync.dma_start(table_scales[32 * q : 32 * q + 4, :].bitcast(I32), x_scales[0, 4 * q : 4 * q + 4, :].bitcast(I32))
-        w2_raw = [load_half(w2, "w2", 0)]
+        for r in range(PACK):
+            nc.sync.dma_start(table_scales[r:P:QUADRANT, :].bitcast(I32), x_scales[0, r : K // BLOCK : PACK, :].bitcast(I32))
+        w2_raw = [load_row_pair(w2, "w2", 0)]
         nc.sync.dma_start(offs_t[:], offs)
-        w2_raw.append(load_half(w2, "w2", 1))
+        w2_raw.append(load_row_pair(w2, "w2", 1))
         nc.sync.dma_start(table_words[:].bitcast(I32), x_words[0].rearrange("p n t -> p (n t)").bitcast(I32))
-        w1_raw = [load_half(w1, "w1", h) for h in range(2)]
+        w1_raw = [load_row_pair(w1, "w1", h) for h in range(2)]
         nc.sync.dma_start(unit_t[:], unit.rearrange("(p t) o -> p (t o)", t=PACK))
         nc.sync.dma_start(s1_t[:], s1)
         nc.sync.dma_start(s2_t[:], s2)
 
-        def deal(raw, name, copies):
+        def deal(raw, name):
             dealt = keep.tile([P, PACK * H], BF16, name=name + "_dealt", align_bytes=64)
             dealt_view = dealt[:].rearrange("p (t m j) -> p m t j", t=PACK, j=PACK)
             for h in range(2):
-                copies[h](dealt_view[:, h * 64 : (h + 1) * 64], raw[h][:].rearrange("p j (m t) -> p m t j", t=PACK))
+                nc.vector.tensor_copy(dealt_view[:, :, :, 2 * h : 2 * h + 2], raw[h][:].rearrange("p j (m t) -> p m t j", t=PACK))
             return dealt
 
         def quantise(dealt, name, pieces):
             codes = keep.tile([P, H], U32, name=name + "_codes", align_bytes=64)
-            plane = keep.tile([P, H], U8, name=name + "_plane", align_bytes=64)
+            scales = keep.tile([P, H], U8, name=name + "_scales", align_bytes=64)
             width = H // pieces
             for i in range(pieces):
                 cols = slice(i * width, (i + 1) * width)
-                nc.vector.quantize_mx(out=codes[:, cols].bitcast(FP8X4), scales=plane[:, cols], in_=dealt[:, i * PACK * width : (i + 1) * PACK * width])
-            return codes, plane
+                nc.vector.quantize_mx(out=codes[:, cols].bitcast(FP8X4), scales=scales[:, cols], in_=dealt[:, i * PACK * width : (i + 1) * PACK * width])
+            return codes, scales
 
-        def product(codes, plane, name):
+        def product(codes, scales, name):
             banks = []
             for t in range(PACK):
                 cols = slice(t * P, (t + 1) * P)
                 bank = psum.tile([P, S], F32, name=name + "_bank", tag=name + "_bank%d" % t)
-                nc.tensor.matmul_mx(out=bank[:], lhsT=codes[:, cols].bitcast(FP8X4), lhsT_scale=plane[:, cols],
-                                    rhs=x_codes[:].bitcast(FP8X4), rhs_scale=x_plane[:], start=True, stop=True)
+                nc.tensor.matmul_mx(out=bank[:], lhsT=codes[:, cols].bitcast(FP8X4), lhsT_scale=scales[:, cols],
+                                    rhs=x_codes[:].bitcast(FP8X4), rhs_scale=x_picked_scales[:], start=True, stop=True)
                 banks.append(bank)
             return banks
 
-        halves = [(slice(h * HALF, (h + 1) * HALF), slice(h * LIST_HALF, (h + 1) * LIST_HALF)) for h in range(2)]
+        def interleaved(words):
+            return words.rearrange("p (c i t) -> p c t i", i=RUN, t=PACK)
 
-        w2_q = quantise(deal(w2_raw, "w2", [nc.scalar.copy, nc.vector.tensor_copy]), "w2", 1)
+        def in_runs(planes):
+            return planes.rearrange("p t (c i) -> p c t i", i=RUN)
+
+        w2_codes, w2_scales = quantise(deal(w2_raw, "w2"), "w2", 1)
         w3_raw = keep.tile([P, PACK, N], F32, name="w3_raw", tag="w2_raw0")
         nc.sync.dma_start(w3_raw[:], w3.rearrange("(p j) n -> p j n", j=PACK))
-        nc.vector.tensor_copy(x_plane[:], table_scales[:].indirect(offs_t[:]))
+        nc.vector.tensor_copy(x_picked_scales[:], table_scales[:].indirect(offs_t[:]))
         nc.vector.tensor_copy(x_codes[:], table_words[:].indirect(offs_t[:]))
-        g_banks = product(w2_q[0], w2_q[1], "w2")
+        gate_banks = product(w2_codes, w2_scales, "w2")
         set1 = []
         for t in range(PACK):
-            set1.append(keep.tile([P, WIN], F32, name="set1_%d" % t))
-            nc.scalar.activation(set1[t][:, :S], g_banks[t][:], ACT.Sigmoid, scale=1.5)
+            set1.append(keep.tile([P, WINDOW], F32, name="set1_%d" % t))
+            nc.scalar.activation(set1[t][:, :S], gate_banks[t][:], ACT.Sigmoid, scale=1.5)
 
-        w1_q = quantise(deal(w1_raw, "w1", [nc.vector.tensor_copy, nc.vector.tensor_copy]), "w1", 2)
-        y_banks = product(w1_q[0], w1_q[1], "w1")
+        w1_codes, w1_scales = quantise(deal(w1_raw, "w1"), "w1", PACK)
+        y_banks = product(w1_codes, w1_scales, "w1")
 
         w3_grouped = keep.tile([P, PACK * N], BF16, name="w3_grouped", align_bytes=64)
         w3_codes = keep.tile([P, N], U32, name="w3_codes", align_bytes=64)
-        w3_plane = keep.tile([P, N], U8, name="w3_plane", align_bytes=64)
-        nc.vector.tensor_copy(w3_grouped[:].rearrange("p (c i t) -> p c t i", i=4, t=PACK),
-                              w3_raw[:].rearrange("p t (c i) -> p c t i", i=4))
+        w3_scales = keep.tile([P, N], U8, name="w3_scales", align_bytes=64)
+        nc.vector.tensor_copy(interleaved(w3_grouped[:]), in_runs(w3_raw[:]))
 
-        y = [keep.tile([P, WIN], F32, name="y%d" % t) for t in range(PACK)]
+        y = [keep.tile([P, WINDOW], F32, name="y%d" % t) for t in range(PACK)]
         y1 = [keep.tile([P, S], F32, name="y1_%d" % t) for t in range(PACK)]
         own = [keep.tile([P, S], F32, name="own%d" % t) for t in range(PACK)]
         taken = [keep.tile([P, S], F32, name="taken%d" % t) for t in range(PACK)]
@@ -133,14 +141,13 @@ def tile_picked_ybenesn_route_p_kernel(tc, x_words, x_scales, w1, w2, unit, w3, 
         copy_y(0)
         copy_y(1)
         make_own(0)
-        make_own(1)
         for t in range(PACK):
             fetch_y(t)
             if t + 2 < PACK:
                 copy_y(t + 2)
+        nc.vector.quantize_mx(out=w3_codes[:].bitcast(FP8X4), scales=w3_scales[:], in_=w3_grouped[:])
         make_taken(0)
-        nc.vector.quantize_mx(out=w3_codes[:].bitcast(FP8X4), scales=w3_plane[:], in_=w3_grouped[:])
-
+        make_own(1)
         make_lay1(0)
         for t in range(1, PACK):
             make_taken(t)
@@ -148,58 +155,54 @@ def tile_picked_ybenesn_route_p_kernel(tc, x_words, x_scales, w1, w2, unit, w3, 
             make_lay1(t)
 
         kept = [keep.tile([P, PACK, HALF], F32, name="kept%d" % h) for h in range(2)]
-        fetched = [keep.tile([P, PACK, HALF], F32, name="fetched0"), keep.tile([P, PACK, HALF], F32, name="fetched1", tag="own3")]
+        fetched = [keep.tile([P, PACK, S - LAST], F32, name="fetched0"),
+                   keep.tile([P, PACK, LAST], F32, name="fetched1", tag="set1_%d" % (PACK - 1))]
+        split = (S - LAST) // PER_COLUMN
+        fetched_entries = [slice(0, split), slice(split, S // PER_COLUMN)]
         set2 = {t: keep.tile([P, S], F32, name="set2_%d" % t, tag="taken%d" % (t - FUSED)) for t in range(FUSED, PACK)}
 
         def make_kept(t, h):
-            cols, entries = halves[h]
-            if t < FUSED:
-                nc.vector.tensor_tensor(kept[h][:, t, :], set1[t][:].indirect(s2_t[:, entries]), lay1[t][:, cols], ALU.mult)
-            else:
-                nc.vector.tensor_tensor(kept[h][:, t, :], set2[t][:, cols], lay1[t][:, cols], ALU.mult)
-
-        def fetch_offered(t, h):
-            nc.scalar.activation(fetched[h][:, t, :], offered[t][:].indirect(s2_t[:, halves[h][1]]), ACT.Copy)
+            cols = slice(h * HALF, (h + 1) * HALF)
+            entries = slice(h * HALF // PER_COLUMN, (h + 1) * HALF // PER_COLUMN)
+            setting = set1[t][:].indirect(s2_t[:, entries]) if t < FUSED else set2[t][:, cols]
+            nc.vector.tensor_tensor(kept[h][:, t, :], setting, lay1[t][:, cols], ALU.mult)
 
         for t in range(FUSED, PACK):
             nc.scalar.activation(set2[t][:], set1[t][:].indirect(s2_t[:]), ACT.Copy)
         make_kept(0, 0)
         make_offered(PACK - 1)
-        for h in range(2):
+        for part in range(2):
             for t in range(PACK):
-                fetch_offered(t, h)
+                nc.scalar.activation(fetched[part][:, t, :], offered[t][:].indirect(s2_t[:, fetched_entries[part]]), ACT.Copy)
         for h in range(2):
             for t in range(PACK):
                 if (t, h) != (0, 0):
                     make_kept(t, h)
 
-        chunks = ((0, 0, 256), (1, 0, 128), (1, 128, 128))
-        hid = [keep.tile([P, PACK * width], BF16, name="hid%d" % c, align_bytes=64) for c, (h, start, width) in enumerate(chunks)]
+        hid = [keep.tile([P, PACK * width], BF16, name="hid%d" % c, align_bytes=64) for c, (start, width) in enumerate(CHUNKS)]
 
         def make_hid(c):
-            h, start, width = chunks[c]
-            cols = slice(start, start + width)
-            nc.vector.tensor_tensor(hid[c][:].rearrange("p (c i t) -> p c t i", i=4, t=PACK),
-                                    kept[h][:, :, cols].rearrange("p t (c i) -> p c t i", i=4),
-                                    fetched[h][:, :, cols].rearrange("p t (c i) -> p c t i", i=4), ALU.subtract)
+            start, width = CHUNKS[c]
+            kept_part = kept[start // HALF][:, :, start % HALF : start % HALF + width]
+            fetched_part = fetched[0][:, :, start : start + width] if start < S - LAST else fetched[1][:]
+            nc.vector.tensor_tensor(interleaved(hid[c][:]), in_runs(kept_part), in_runs(fetched_part), ALU.subtract)
 
         def finish(c):
-            h, start, width = chunks[c]
-            cols = slice(h * HALF + start, h * HALF + start + width)
-            h_codes = keep.tile([P, width], U32, name="h_codes%d" % c, align_bytes=64)
-            h_plane = keep.tile([P, width], U8, name="h_plane%d" % c, align_bytes=64)
-            nc.vector.quantize_mx(out=h_codes[:].bitcast(FP8X4), scales=h_plane[:], in_=hid[c][:])
-            bank = psum.tile([P, 2, width], F32, name="out_bank", tag="w2_bank%d" % c)
-            for a in range(2):
-                rows = slice(a * P, (a + 1) * P)
-                nc.tensor.matmul_mx(out=bank[:, a, :], lhsT=w3_codes[:, rows].bitcast(FP8X4), lhsT_scale=w3_plane[:, rows],
-                                    rhs=h_codes[:].bitcast(FP8X4), rhs_scale=h_plane[:], start=True, stop=True)
-            res = keep.tile([P, 2, width], F32, name="res%d" % c)
-            nc.scalar.copy(res[:], bank[:])
-            nc.sync.dma_start(out.rearrange("(a p) j -> p a j", p=P)[:, :, cols], res[:])
+            start, width = CHUNKS[c]
+            hid_codes = keep.tile([P, width], U32, name="hid_codes%d" % c, align_bytes=64)
+            hid_scales = keep.tile([P, width], U8, name="hid_scales%d" % c, align_bytes=64)
+            nc.vector.quantize_mx(out=hid_codes[:].bitcast(FP8X4), scales=hid_scales[:], in_=hid[c][:])
+            bank = psum.tile([P, N // P, width], F32, name="out_bank", tag="w2_bank%d" % c)
+            for a in range(N // P):
+                features = slice(a * P, (a + 1) * P)
+                nc.tensor.matmul_mx(out=bank[:, a, :], lhsT=w3_codes[:, features].bitcast(FP8X4), lhsT_scale=w3_scales[:, features],
+                                    rhs=hid_codes[:].bitcast(FP8X4), rhs_scale=hid_scales[:], start=True, stop=True)
+            result = keep.tile([P, N // P, width], F32, name="result%d" % c)
+            nc.scalar.copy(result[:], bank[:])
+            nc.sync.dma_start(out.rearrange("(a p) j -> p a j", p=P)[:, :, start : start + width], result[:])
 
         make_hid(0)
-        for c in range(1, len(chunks)):
+        for c in range(1, len(CHUNKS)):
             make_hid(c)
             finish(c - 1)
-        finish(len(chunks) - 1)
+        finish(len(CHUNKS) - 1)

from contextlib import ExitStack

import concourse.mybir as mybir

K, T, S, N, H = 512, 2048, 512, 256, 512
FLOPS = 2 * K * H * S * 2 + 2 * H * N * S

F32 = mybir.dt.float32
BF16 = mybir.dt.bfloat16
I32 = mybir.dt.int32
U32 = mybir.dt.uint32
U16 = mybir.dt.uint16
U8 = mybir.dt.uint8
FP8X4 = mybir.dt.float8_e4m3fn_x4
ACT = mybir.ActivationFunctionType
ALU = mybir.AluOpType

P = 128
PACK = 4
BLOCK = 32
QUADRANT = 32
PER_COLUMN = 16
RUN = 4
HALF = S // 2
WINDOW = S + PER_COLUMN
FUSED = 2
LAST = 128
CHUNKS = ((0, HALF), (HALF, HALF - LAST), (S - LAST, LAST))


def tile_picked_ybenesn_route_p_kernel(tc, x_words, x_scales, w1, w2, unit, w3, offs, s1, s2, out):
    nc = tc.nc
    with ExitStack() as ctx:
        keep = ctx.enter_context(tc.tile_pool(name="keep", bufs=1))
        psum = ctx.enter_context(tc.psum_pool(name="psum", bufs=1))

        offs_t = keep.tile([P, S // PER_COLUMN], U16, name="offs_t")
        s1_t = keep.tile([P, S // PER_COLUMN], U16, name="s1_t")
        s2_t = keep.tile([P, S // PER_COLUMN], U16, name="s2_t")
        unit_t = keep.tile([P, PACK], F32, name="unit_t")
        table_words = keep.tile([P, T], U32, name="table_words", align_bytes=64)
        table_scales = keep.tile([P, T], U8, name="table_scales", align_bytes=64)
        x_codes = keep.tile([P, S], U32, name="x_codes", align_bytes=64)
        x_picked_scales = keep.tile([P, S], U8, name="x_picked_scales", align_bytes=64)

        def load_row_pair(w, name, h):
            raw = keep.tile([P, 2, H], F32, name=name + "_raw%d" % h)
            nc.sync.dma_start(raw[:], w.rearrange("(p j) c -> p j c", j=PACK)[:, 2 * h : 2 * h + 2, :])
            return raw

        nc.vector.memset(table_scales[:].bitcast(I32), 0)
        for r in range(PACK):
            nc.sync.dma_start(table_scales[r:P:QUADRANT, :].bitcast(I32), x_scales[0, r : K // BLOCK : PACK, :].bitcast(I32))
        w2_raw = [load_row_pair(w2, "w2", 0)]
        nc.sync.dma_start(offs_t[:], offs)
        w2_raw.append(load_row_pair(w2, "w2", 1))
        nc.sync.dma_start(table_words[:].bitcast(I32), x_words[0].rearrange("p n t -> p (n t)").bitcast(I32))
        w1_raw = [load_row_pair(w1, "w1", h) for h in range(2)]
        nc.sync.dma_start(unit_t[:], unit.rearrange("(p t) o -> p (t o)", t=PACK))
        nc.sync.dma_start(s1_t[:], s1)
        nc.sync.dma_start(s2_t[:], s2)

        def deal(raw, name):
            dealt = keep.tile([P, PACK * H], BF16, name=name + "_dealt", align_bytes=64)
            dealt_view = dealt[:].rearrange("p (t m j) -> p m t j", t=PACK, j=PACK)
            for h in range(2):
                nc.vector.tensor_copy(dealt_view[:, :, :, 2 * h : 2 * h + 2], raw[h][:].rearrange("p j (m t) -> p m t j", t=PACK))
            return dealt

        def quantise(dealt, name, pieces):
            codes = keep.tile([P, H], U32, name=name + "_codes", align_bytes=64)
            scales = keep.tile([P, H], U8, name=name + "_scales", align_bytes=64)
            width = H // pieces
            for i in range(pieces):
                cols = slice(i * width, (i + 1) * width)
                nc.vector.quantize_mx(out=codes[:, cols].bitcast(FP8X4), scales=scales[:, cols], in_=dealt[:, i * PACK * width : (i + 1) * PACK * width])
            return codes, scales

        def product(codes, scales, name):
            banks = []
            for t in range(PACK):
                cols = slice(t * P, (t + 1) * P)
                bank = psum.tile([P, S], F32, name=name + "_bank", tag=name + "_bank%d" % t)
                nc.tensor.matmul_mx(out=bank[:], lhsT=codes[:, cols].bitcast(FP8X4), lhsT_scale=scales[:, cols],
                                    rhs=x_codes[:].bitcast(FP8X4), rhs_scale=x_picked_scales[:], start=True, stop=True)
                banks.append(bank)
            return banks

        def interleaved(words):
            return words.rearrange("p (c i t) -> p c t i", i=RUN, t=PACK)

        def in_runs(planes):
            return planes.rearrange("p t (c i) -> p c t i", i=RUN)

        w2_codes, w2_scales = quantise(deal(w2_raw, "w2"), "w2", 1)
        w3_raw = keep.tile([P, PACK, N], F32, name="w3_raw", tag="w2_raw0")
        nc.sync.dma_start(w3_raw[:], w3.rearrange("(p j) n -> p j n", j=PACK))
        nc.vector.tensor_copy(x_picked_scales[:], table_scales[:].indirect(offs_t[:]))
        nc.vector.tensor_copy(x_codes[:], table_words[:].indirect(offs_t[:]))
        gate_banks = product(w2_codes, w2_scales, "w2")
        set1 = []
        for t in range(PACK):
            set1.append(keep.tile([P, WINDOW], F32, name="set1_%d" % t))
            nc.scalar.activation(set1[t][:, :S], gate_banks[t][:], ACT.Sigmoid, scale=1.5)

        w1_codes, w1_scales = quantise(deal(w1_raw, "w1"), "w1", PACK)
        y_banks = product(w1_codes, w1_scales, "w1")

        w3_grouped = keep.tile([P, PACK * N], BF16, name="w3_grouped", align_bytes=64)
        w3_codes = keep.tile([P, N], U32, name="w3_codes", align_bytes=64)
        w3_scales = keep.tile([P, N], U8, name="w3_scales", align_bytes=64)
        nc.vector.tensor_copy(interleaved(w3_grouped[:]), in_runs(w3_raw[:]))

        y = [keep.tile([P, WINDOW], F32, name="y%d" % t) for t in range(PACK)]
        y1 = [keep.tile([P, S], F32, name="y1_%d" % t) for t in range(PACK)]
        own = [keep.tile([P, S], F32, name="own%d" % t) for t in range(PACK)]
        taken = [keep.tile([P, S], F32, name="taken%d" % t) for t in range(PACK)]
        lay1 = [keep.tile([P, S], F32, name="lay1_%d" % t) for t in range(PACK)]
        offered = [keep.tile([P, S], F32, name="offered%d" % t) for t in range(PACK)]

        def copy_y(t):
            nc.scalar.activation(y[t][:, :S], y_banks[t][:], ACT.Copy, scale=unit_t[:, t : t + 1])

        def fetch_y(t):
            nc.scalar.activation(y1[t][:], y[t][:].indirect(s1_t[:]), ACT.Copy)

        def make_own(t):
            nc.vector.scalar_tensor_tensor(own[t][:], y_banks[t][:], unit_t[:, t : t + 1], set1[t][:, :S], ALU.mult, ALU.mult)

        def make_taken(t):
            nc.vector.scalar_tensor_tensor(taken[t][:], set1[t][:, :S], 1.0, y1[t][:], ALU.subtract, ALU.mult)

        def make_lay1(t):
            nc.vector.tensor_tensor(lay1[t][:], own[t][:], taken[t][:], ALU.subtract)

        def make_offered(t):
            nc.vector.scalar_tensor_tensor(offered[t][:], set1[t][:, :S], 1.0, lay1[t][:], ALU.subtract, ALU.mult)

        make_own(2)
        make_own(3)
        copy_y(0)
        copy_y(1)
        make_own(0)
        for t in range(PACK):
            fetch_y(t)
            if t + 2 < PACK:
                copy_y(t + 2)
        nc.vector.quantize_mx(out=w3_codes[:].bitcast(FP8X4), scales=w3_scales[:], in_=w3_grouped[:])
        make_taken(0)
        make_own(1)
        make_lay1(0)
        for t in range(1, PACK):
            make_taken(t)
            make_offered(t - 1)
            make_lay1(t)

        kept = [keep.tile([P, PACK, HALF], F32, name="kept%d" % h) for h in range(2)]
        fetched = [keep.tile([P, PACK, S - LAST], F32, name="fetched0"),
                   keep.tile([P, PACK, LAST], F32, name="fetched1", tag="set1_%d" % (PACK - 1))]
        split = (S - LAST) // PER_COLUMN
        fetched_entries = [slice(0, split), slice(split, S // PER_COLUMN)]
        set2 = {t: keep.tile([P, S], F32, name="set2_%d" % t, tag="taken%d" % (t - FUSED)) for t in range(FUSED, PACK)}

        def make_kept(t, h):
            cols = slice(h * HALF, (h + 1) * HALF)
            entries = slice(h * HALF // PER_COLUMN, (h + 1) * HALF // PER_COLUMN)
            setting = set1[t][:].indirect(s2_t[:, entries]) if t < FUSED else set2[t][:, cols]
            nc.vector.tensor_tensor(kept[h][:, t, :], setting, lay1[t][:, cols], ALU.mult)

        for t in range(FUSED, PACK):
            nc.scalar.activation(set2[t][:], set1[t][:].indirect(s2_t[:]), ACT.Copy)
        make_kept(0, 0)
        make_offered(PACK - 1)
        for part in range(2):
            for t in range(PACK):
                nc.scalar.activation(fetched[part][:, t, :], offered[t][:].indirect(s2_t[:, fetched_entries[part]]), ACT.Copy)
        for h in range(2):
            for t in range(PACK):
                if (t, h) != (0, 0):
                    make_kept(t, h)

        hid = [keep.tile([P, PACK * width], BF16, name="hid%d" % c, align_bytes=64) for c, (start, width) in enumerate(CHUNKS)]

        def make_hid(c):
            start, width = CHUNKS[c]
            kept_part = kept[start // HALF][:, :, start % HALF : start % HALF + width]
            fetched_part = fetched[0][:, :, start : start + width] if start < S - LAST else fetched[1][:]
            nc.vector.tensor_tensor(interleaved(hid[c][:]), in_runs(kept_part), in_runs(fetched_part), ALU.subtract)

        def finish(c):
            start, width = CHUNKS[c]
            hid_codes = keep.tile([P, width], U32, name="hid_codes%d" % c, align_bytes=64)
            hid_scales = keep.tile([P, width], U8, name="hid_scales%d" % c, align_bytes=64)
            nc.vector.quantize_mx(out=hid_codes[:].bitcast(FP8X4), scales=hid_scales[:], in_=hid[c][:])
            bank = psum.tile([P, N // P, width], F32, name="out_bank", tag="w2_bank%d" % c)
            for a in range(N // P):
                features = slice(a * P, (a + 1) * P)
                nc.tensor.matmul_mx(out=bank[:, a, :], lhsT=w3_codes[:, features].bitcast(FP8X4), lhsT_scale=w3_scales[:, features],
                                    rhs=hid_codes[:].bitcast(FP8X4), rhs_scale=hid_scales[:], start=True, stop=True)
            result = keep.tile([P, N // P, width], F32, name="result%d" % c)
            nc.scalar.copy(result[:], bank[:])
            nc.sync.dma_start(out.rearrange("(a p) j -> p a j", p=P)[:, :, start : start + width], result[:])

        make_hid(0)
        for c in range(1, len(CHUNKS)):
            make_hid(c)
            finish(c - 1)
        finish(len(CHUNKS) - 1)
